import numpy as np, ml_dtypes
CORES = [16,18,20,22]
N = 4
import mx_ref
BF = ml_dtypes.bfloat16
def entries(a):
    return np.ascontiguousarray(a.T).reshape(-1)
def table(e):
    return np.ascontiguousarray(np.reshape(e, (-1, 16)).T).astype(np.int32)
def cut(t, i, w=512):
    return t[:, w * i:w * i + w]
def decode(q):
    o = []
    for b in range(4):
        e = np.zeros((128, 128, 4), np.float32); e[np.arange(128), np.arange(128), b] = 1
        o.append(mx_ref.matmul(mx_ref.quantize(e.reshape(128, 512).astype(BF)), q))
    return np.stack(o, axis=2).reshape(128, -1)
def f(rng, *shape):
    return mx_ref.flush((rng.standard_normal(shape, dtype=np.float32) * np.exp2(rng.integers(-2, 3, shape[:-1] + (1,)))).astype(BF))
def wide(rng, *shape, cols=0):
    v = rng.standard_normal(shape, dtype=np.float32) * np.exp2(rng.integers(-12, 13, shape)).astype(np.float32)
    if cols: v *= np.repeat(np.exp2(rng.integers(-cols, cols + 1, shape[:-2] + (1, shape[-1] // 4))) * (rng.random(shape[:-2] + (1, shape[-1] // 4)) > 0.0625), 4, axis=-1).astype(np.float32)
    return mx_ref.flush(v.astype(BF))
T, K, O = 512, 512, 2
HA = (1237, 1811, 947, 1543)
HB = (40503, 12289, 58111, 3571)
def setup_inputs(rng):
    return {"tb": f(rng, N, 128, 4 * K), "ids": np.stack([table(rng.integers(0, 4096, T)) for r in range(N)]), "w": f(rng, N, 128, 512 * O)}
def setup_inputs_alike(rng):
    d = setup_inputs(rng); e = rng.integers(0, 4096, T)
    d["ids"] = np.stack([table(e) for r in range(N)]); return d
def setup_inputs_ends(rng):
    d = setup_inputs(rng); o = []
    for r in range(N):
        e = rng.choice([0, 4095], T); e[rng.permutation(T)[:2]] = [0, 4095]
        o.append(table(e))
    d["ids"] = np.stack(o); return d
def setup_inputs_order(rng):
    d = setup_inputs(rng); t = rng.standard_normal((N, 128, 4 * K), dtype=np.float32)
    one = rng.permutation(np.concatenate([np.arange(N), rng.integers(0, N, 16 - N)]))
    for g in range(16):
        p = int(one[g]); o = int(rng.choice([q for q in range(N) if abs(q - p) >= 2]))
        size = np.float32(2.0 ** int(rng.integers(0, 3)))
        X = np.tile(rng.choice([-1, 1], (8, 4)).astype(np.float32) * size, (1, K))
        v = t[:, 8 * g:8 * g + 8]; v *= size * np.float32(2.0 ** -14)
        v[min(p, o)] = X; v[max(p, o)] = -X
    d["tb"] = mx_ref.flush(t.astype(BF)); return d
def setup_inputs_same(rng):
    d = setup_inputs(rng)
    d["ids"] = np.stack([table(np.full(T, rng.integers(0, 4096))) for r in range(N)]); return d
def setup_inputs_spread(rng):
    d = setup_inputs(rng); d["tb"] = wide(rng, N, 128, 4 * K, cols=8); return d
def check_inputs(d):
    b = []
    for r in range(N):
        e = entries(d["ids"][r])
        if e.min() < 0 or e.max() > 4095: b.append("ids")
    return b
def address(q, e):
    return ((e * HA[q] + HB[q]) >> 5) & (K - 1)
def reference(tb, ids, w):
    d = [decode(mx_ref.quantize(tb[q])).reshape(128, -1, 4) for q in range(N)]
    y = np.zeros((N, 128, O * T), np.float32)
    for r in range(N):
        e = entries(ids[r])
        v = d[0][:, address(0, e)]
        for q in range(1, N): v = v + d[q][:, address(q, e)]
        V = mx_ref.quantize(np.ascontiguousarray(v.reshape(128, -1)).astype(BF))
        for o in range(O): y[r][:, T * o:T * o + T] = mx_ref.matmul(mx_ref.quantize(np.ascontiguousarray(cut(w[r], o))), V)
    return {"y": y}

@@ -1,0 +1,232 @@
+from concourse.bass import DstId, RemoteDMATransfer
+from concourse.mybir import dt, AluOpType, ActivationFunctionType
+
+N, TOK, K, O = 4, 512, 512, 2
+HA = (1237, 1811, 947, 1543)
+HB = (40503, 12289, 58111, 3571)
+COPY = ActivationFunctionType.Copy
+CFG = {
+    "CH": [(0, 320), (320, 512)],
+    "XOR": (2, 3, 1),
+    "NV": [[2, 2, 2], [2, 2, 2]],
+    "DEINT": False,
+}
+
+SCRATCH = {
+    "ids8": ("sbuf", [128, 32], "int32"),
+    "lst": ("sbuf", [128, 96], "int32"),
+    "hx": ("sbuf", [128, 128], "int32"),
+    "hh": ("sbuf", [128, 128], "int32"),
+    "tbt": ("sbuf", [128, 4 * K], "bfloat16"),
+    "tbd": ("sbuf", [128, 4 * K], "bfloat16"),
+    "wt": ("sbuf", [128, 512 * O], "bfloat16"),
+    "wq": ("sbuf", [128, 128 * O], "float8_e4m3fn_x4"),
+    "wp": ("sbuf", [128, 128 * O], "uint8"),
+    "one": ("sbuf", [128, 128], "bfloat16"),
+    "eye": ("sbuf", [128, 128], "bfloat16"),
+    "e": ("sbuf", [128, 2048], "bfloat16"),
+    "eq": ("sbuf", [128, 512], "float8_e4m3fn_x4"),
+    "ep": ("sbuf", [128, 512], "uint8"),
+    "vt": ("sbuf", [128, 4 * TOK], "bfloat16"),
+    "vq": ("sbuf", [128, TOK], "float8_e4m3fn_x4"),
+    "vp": ("sbuf", [128, TOK], "uint8"),
+    "yt": ("sbuf", [128, O * TOK], "float32"),
+}
+for _t in range(4):
+    SCRATCH["off%d" % _t] = ("sbuf", [128, 128], "uint16")
+for _s in range(4):
+    SCRATCH["gt%d" % _s] = ("sbuf", [128, 4 * TOK], "bfloat16")
+    SCRATCH["gq%d" % _s] = ("sbuf", [128, TOK], "float8_e4m3fn_x4")
+    SCRATCH["gp%d" % _s] = ("sbuf", [128, TOK], "uint8")
+for _s in range(1, 4):
+    SCRATCH["rq%d" % _s] = ("sbuf", [128, TOK], "float8_e4m3fn_x4")
+    SCRATCH["rp%d" % _s] = ("sbuf", [128, TOK], "uint8")
+for _b in range(8):
+    SCRATCH["ps%d" % _b] = ("psum", [128, 512], "float32")
+
+SEMAPHORES = ["sv", "ss", "sp", "sg", "li", "lt", "lw", "ly", "sent"] + \
+    ["la%d" % s for s in range(3)] + ["ar%d%d" % (s, c) for s in range(3) for c in range(4)]
+
+
+def rank_program(g, core, T, topo):
+    r = T.rank_of(core)
+    if r is None:
+        return
+    CH, XOR = CFG["CH"], CFG["XOR"]
+    V, S, P, Y = g.vector, g.scalar, g.tensor, g.sync
+    Q = {"v": V, "s": S, "p": P, "g": g, "y": Y}
+    peer = [r ^ XOR[s] for s in range(3)]
+    pcore = [T.cores[p] for p in peer]
+    eng = [topo.engines(core, c) for c in pcore]
+    done, seen, local = {}, {}, [0]
+
+    def fin(sem, ins, n=1):
+        ins.then_inc(T.sem[sem], n)
+        done[sem] = done.get(sem, 0) + n
+        return (sem, done[sem])
+
+    def need(q, *marks):
+        for sem, n in marks:
+            if seen.get((q, sem), 0) < n:
+                Q[q].wait_ge(T.sem[sem], n)
+                seen[(q, sem)] = n
+
+    def send(items):
+        tr = []
+        for s, es, src, dst, sem in items:
+            rid, pid, _ = topo.addr(pcore[s])
+            tr.append(RemoteDMATransfer(dst_ids=[DstId(rid=rid, pnc=pid)], dma_engine_mask=sum(1 << e for e in es),
+                                        remote_sem=T.sem[sem], srcs=[src], dsts=[dst]))
+            local[0] += len(es)
+        g.remote_dma_fused(tr, local_sem=T.sem.sent)
+
+    for i in range(4):
+        fin("li", Y.dma_start(T.ids8[16 * i:16 * i + 16, :], T.ids[:, :]), 16)
+        j = i + 4
+        m_ids = fin("li", S.dma_start(T.ids8[16 * j:16 * j + 16, :], T.ids[:, :]), 16)
+    m_tb = fin("lt", Y.dma_start(T.tbt[:], T.tb[:, :]), 16)
+    m_w = fin("lw", Y.dma_start(T.wt[:], T.w[:, :]), 16)
+
+    m_one = fin("sv", V.memset(T.one[:], 1.0))
+    need("g", m_one)
+    m_eye = fin("sg", g.affine_select(T.eye[:], T.one[:], [[-1, 128]], AluOpType.is_equal, 0.0, 0, 1))
+    m = fin("sv", V.memset(T.e[:], 0.0))
+    need("v", m, m_eye)
+    for b in range(4):
+        m = fin("sv", V.tensor_copy(T.e[:, 512 * b + b:512 * b + 512:4], T.eye[:]))
+    need("v", m)
+    m_e = fin("sv", V.quantize_mx(T.eq[:], T.ep[:], T.e[:]))
+
+    need("g", m_ids)
+    lists = [(s, es, T.ids8[:], T.lst[:, 32 * s:32 * s + 32], "la%d" % s)
+             for s, es in enumerate((eng[0][0:8], eng[1][8:12], eng[2][12:16]))]
+    send(lists[0:1])
+    send(lists[1:3])
+    m_la = [(x[4], len(x[1])) for x in lists]
+
+    m_off = {}
+
+    def hashes(src, b0, b1, order):
+        c0, c1 = 32 * b0, 32 * b1
+        x, h = T.hx[:, c0:c1], T.hh[:, c0:c1]
+        need("v", fin("sv", V.tensor_scalar(x, src, HA[r], HB[r], AluOpType.mult, AluOpType.add)))
+        if CFG["DEINT"]:
+            need("v", fin("sv", V.tensor_scalar(h, x, 5, K - 1, AluOpType.logical_shift_right, AluOpType.bitwise_and)))
+            m3 = fin("sv", V.tensor_copy(T.off0[:, c0:c1], h))
+            for k in range(b0, b1):
+                for t in range(4):
+                    m_off[k, t] = m3
+            return
+        need("v", fin("sv", V.tensor_scalar(h, x, 3, 4 * (K - 1), AluOpType.logical_shift_right, AluOpType.bitwise_and)))
+        for t in order:
+            m3 = fin("sv", V.tensor_scalar(T["off%d" % t][:, c0:c1], h, t, None, AluOpType.add))
+            for k in range(b0, b1):
+                m_off[k, t] = m3
+
+    def gather(k, c, nv):
+        a, z = CH[c]
+        o = 32 * k
+        marks = []
+        for t in range(4):
+            out = T["gt%d" % k][:, 4 * a + t:4 * z:4]
+            win, off = (T.tbd[:, K * t:K * t + K], T.off0) if CFG["DEINT"] else (T.tbt[:], T["off%d" % t])
+            src = win.indirect(off[:, o + a // 16:o + z // 16])
+            if t < nv:
+                need("v", m_win[t], m_off[k, t])
+                marks.append(fin("sv", V.tensor_copy(out, src)))
+            else:
+                need("s", m_win[t], m_off[k, t])
+                marks.append(fin("ss", S.activation(out, src, COPY)))
+        return marks
+
+    def pack(k, c, marks):
+        a, z = CH[c]
+        need("v", *marks)
+        return fin("sv", V.quantize_mx(T["gq%d" % k][:, a:z], T["gp%d" % k][:, a:z], T["gt%d" % k][:, 4 * a:4 * z]))
+
+    m_own = {}
+    need("v", m_ids)
+    hashes(T.ids8[:], 0, 1, (2, 3, 0, 1))
+    m_win = [m_tb] * 4
+    if CFG["DEINT"]:
+        need("v", m_tb)
+        need("s", m_tb)
+        m_win = [fin("sv", V.tensor_copy(T.tbd[:, K * t:K * t + K], T.tbt[:, t:4 * K:4])) for t in range(3)] + \
+                [fin("ss", S.activation(T.tbd[:, K * t:K * t + K], T.tbt[:, t:4 * K:4], COPY)) for t in range(3, 4)]
+    early = len(CH) - 1
+    for c in range(early):
+        m_own[c] = pack(0, c, gather(0, c, 2))
+    need("v", m_w)
+    m_wq = fin("sv", V.quantize_mx(T.wq[:], T.wp[:], T.wt[:]))
+
+    arr = {}
+    for c, (a, z) in enumerate(CH):
+        for s in range(3):
+            k = s + 1
+            if c == 0 and s == 0:
+                need("v", m_la[0])
+                hashes(T.lst[:, 0:32], 1, 2, (3, 2, 1, 0))
+            marks = gather(k, c, CFG["NV"][c][s])
+            if c == 0 and s == 0:
+                need("v", m_la[1], m_la[2])
+                hashes(T.lst[:, 32:96], 2, 4, (3, 2, 1, 0))
+            need("g", pack(k, c, marks))
+            sem = "ar%d%d" % (s, c)
+            send([(s, eng[s], T["gq%d" % k][:, a:z].bitcast(dt.uint8), T["rq%d" % k][:, a:z].bitcast(dt.uint8), sem)])
+            send([(s, eng[s], T["gp%d" % k][:, a:z], T["rp%d" % k][:, a:z], sem)])
+            arr[s, c] = (sem, 2 * len(eng[s]))
+    for c in range(early, len(CH)):
+        m_own[c] = pack(0, c, gather(0, c, 2))
+
+    order = [1, 0, 2, 3] if (r == 1 or r == 3) else [0, 1, 2, 3]
+    free = {}
+    for c, (a, z) in enumerate(CH):
+        n = z - a
+        base = 4 * (c % 2)
+        last = {}
+        for i, q in enumerate(order):
+            if q == r:
+                cq, cp, mk = T.gq0, T.gp0, m_own[c]
+            else:
+                s = peer.index(q)
+                cq, cp, mk = T["rq%d" % (s + 1)], T["rp%d" % (s + 1)], arr[s, c]
+            need("p", m_e, mk)
+            for b in range(4):
+                if i == 0 and base + b in free:
+                    need("p", free[base + b])
+                last[b] = fin("sp", P.matmul_mx(T["ps%d" % (base + b)][:, 0:n], T.eq[:, 128 * b:128 * b + 128],
+                                                T.ep[:, 128 * b:128 * b + 128], cq[:, a:z], cp[:, a:z], i == 0, i == 3))
+        mv = []
+        for b in range(4):
+            out, src = T.vt[:, 4 * a + b:4 * z:4], T["ps%d" % (base + b)][:, 0:n]
+            if b % 2 == 0:
+                need("v", last[b])
+                mv.append(fin("sv", V.tensor_copy(out, src)))
+            else:
+                need("s", last[b])
+                mv.append(fin("ss", S.activation(out, src, COPY)))
+            free[base + b] = mv[-1]
+        need("v", *mv)
+        m_vq = fin("sv", V.quantize_mx(T.vq[:, a:z], T.vp[:, a:z], T.vt[:, 4 * a:4 * z]))
+        need("p", m_wq, m_vq)
+        my = []
+        for o in range(O):
+            my.append(fin("sp", P.matmul_mx(T["ps%d" % (base + o)][:, 0:n], T.wq[:, 128 * o:128 * o + 128],
+                                            T.wp[:, 128 * o:128 * o + 128], T.vq[:, a:z], T.vp[:, a:z], True, True)))
+        for o in range(O):
+            lo = TOK * o + a
+            out, src = T.yt[:, lo:lo + n], T["ps%d" % (base + o)][:, 0:n]
+            if o == 0:
+                need("v", my[o])
+                mk = fin("sv", V.tensor_copy(out, src))
+                dq = "y"
+            else:
+                need("s", my[o])
+                mk = fin("ss", S.activation(out, src, COPY))
+                dq = "s" if c == len(CH) - 1 else "y"
+            free[base + o] = mk
+            need(dq, mk)
+            fin("ly", Q[dq].dma_start(T.y[:, lo:lo + n], T.yt[:, lo:lo + n]), 16)
+    g.wait_ge(T.sem.sent, local[0])
+    for sem in ("sv", "ss", "sp", "sg", "ly"):
+        need("g", (sem, done[sem]))

@@ -8,8 +8,9 @@ COPY = ActivationFunctionType.Copy
 CFG = {
     "CH": [(0, 320), (320, 512)],
     "XOR": (2, 3, 1),
-    "NV": [[2, 2, 2], [2, 2, 2]],
-    "DEINT": False,
+    "NV": [[2, 2, 2], [2, 2, 1]],
+    "OV": [2, 1],
+    "WLAG": 2,
 }
 
 SCRATCH = {
@@ -18,7 +19,6 @@ SCRATCH = {
     "hx": ("sbuf", [128, 128], "int32"),
     "hh": ("sbuf", [128, 128], "int32"),
     "tbt": ("sbuf", [128, 4 * K], "bfloat16"),
-    "tbd": ("sbuf", [128, 4 * K], "bfloat16"),
     "wt": ("sbuf", [128, 512 * O], "bfloat16"),
     "wq": ("sbuf", [128, 128 * O], "float8_e4m3fn_x4"),
     "wp": ("sbuf", [128, 128 * O], "uint8"),
@@ -110,13 +110,6 @@ def rank_program(g, core, T, topo):
         c0, c1 = 32 * b0, 32 * b1
         x, h = T.hx[:, c0:c1], T.hh[:, c0:c1]
         need("v", fin("sv", V.tensor_scalar(x, src, HA[r], HB[r], AluOpType.mult, AluOpType.add)))
-        if CFG["DEINT"]:
-            need("v", fin("sv", V.tensor_scalar(h, x, 5, K - 1, AluOpType.logical_shift_right, AluOpType.bitwise_and)))
-            m3 = fin("sv", V.tensor_copy(T.off0[:, c0:c1], h))
-            for k in range(b0, b1):
-                for t in range(4):
-                    m_off[k, t] = m3
-            return
         need("v", fin("sv", V.tensor_scalar(h, x, 3, 4 * (K - 1), AluOpType.logical_shift_right, AluOpType.bitwise_and)))
         for t in order:
             m3 = fin("sv", V.tensor_scalar(T["off%d" % t][:, c0:c1], h, t, None, AluOpType.add))
@@ -129,13 +122,12 @@ def rank_program(g, core, T, topo):
         marks = []
         for t in range(4):
             out = T["gt%d" % k][:, 4 * a + t:4 * z:4]
-            win, off = (T.tbd[:, K * t:K * t + K], T.off0) if CFG["DEINT"] else (T.tbt[:], T["off%d" % t])
-            src = win.indirect(off[:, o + a // 16:o + z // 16])
+            src = T.tbt[:].indirect(T["off%d" % t][:, o + a // 16:o + z // 16])
             if t < nv:
-                need("v", m_win[t], m_off[k, t])
+                need("v", m_tb, m_off[k, t])
                 marks.append(fin("sv", V.tensor_copy(out, src)))
             else:
-                need("s", m_win[t], m_off[k, t])
+                need("s", m_tb, m_off[k, t])
                 marks.append(fin("ss", S.activation(out, src, COPY)))
         return marks
 
@@ -147,17 +139,9 @@ def rank_program(g, core, T, topo):
     m_own = {}
     need("v", m_ids)
     hashes(T.ids8[:], 0, 1, (2, 3, 0, 1))
-    m_win = [m_tb] * 4
-    if CFG["DEINT"]:
-        need("v", m_tb)
-        need("s", m_tb)
-        m_win = [fin("sv", V.tensor_copy(T.tbd[:, K * t:K * t + K], T.tbt[:, t:4 * K:4])) for t in range(3)] + \
-                [fin("ss", S.activation(T.tbd[:, K * t:K * t + K], T.tbt[:, t:4 * K:4], COPY)) for t in range(3, 4)]
     early = len(CH) - 1
     for c in range(early):
-        m_own[c] = pack(0, c, gather(0, c, 2))
-    need("v", m_w)
-    m_wq = fin("sv", V.quantize_mx(T.wq[:], T.wp[:], T.wt[:]))
+        m_own[c] = pack(0, c, gather(0, c, CFG["OV"][c]))
 
     arr = {}
     for c, (a, z) in enumerate(CH):
@@ -174,59 +158,75 @@ def rank_program(g, core, T, topo):
             sem = "ar%d%d" % (s, c)
             send([(s, eng[s], T["gq%d" % k][:, a:z].bitcast(dt.uint8), T["rq%d" % k][:, a:z].bitcast(dt.uint8), sem)])
             send([(s, eng[s], T["gp%d" % k][:, a:z], T["rp%d" % k][:, a:z], sem)])
-            arr[s, c] = (sem, 2 * len(eng[s]))
+            arr[peer[s], c] = (sem, 2 * len(eng[s]))
     for c in range(early, len(CH)):
-        m_own[c] = pack(0, c, gather(0, c, 2))
+        m_own[c] = pack(0, c, gather(0, c, CFG["OV"][c]))
+    need("v", m_w)
+    m_wq = fin("sv", V.quantize_mx(T.wq[:], T.wp[:], T.wt[:]))
 
     order = [1, 0, 2, 3] if (r == 1 or r == 3) else [0, 1, 2, 3]
-    free = {}
-    for c, (a, z) in enumerate(CH):
-        n = z - a
-        base = 4 * (c % 2)
-        last = {}
-        for i, q in enumerate(order):
-            if q == r:
-                cq, cp, mk = T.gq0, T.gp0, m_own[c]
-            else:
-                s = peer.index(q)
-                cq, cp, mk = T["rq%d" % (s + 1)], T["rp%d" % (s + 1)], arr[s, c]
-            need("p", m_e, mk)
-            for b in range(4):
-                if i == 0 and base + b in free:
-                    need("p", free[base + b])
-                last[b] = fin("sp", P.matmul_mx(T["ps%d" % (base + b)][:, 0:n], T.eq[:, 128 * b:128 * b + 128],
-                                                T.ep[:, 128 * b:128 * b + 128], cq[:, a:z], cp[:, a:z], i == 0, i == 3))
+    free, last, m_vq, my = {}, {}, {}, {}
+
+    def decode(c, i):
+        (a, z), q, base = CH[c], order[i], 4 * (c % 2)
+        k = 0 if q == r else peer.index(q) + 1
+        cq, cp, mk = (T.gq0, T.gp0, m_own[c]) if q == r else (T["rq%d" % k], T["rp%d" % k], arr[q, c])
+        need("p", m_e, mk)
+        for b in range(4):
+            if i == 0 and base + b in free:
+                need("p", free[base + b])
+            last[c, b] = fin("sp", P.matmul_mx(T["ps%d" % (base + b)][:, 0:z - a], T.eq[:, 128 * b:128 * b + 128],
+                                               T.ep[:, 128 * b:128 * b + 128], cq[:, a:z], cp[:, a:z], i == 0, i == 3))
+
+    def tile(c):
+        (a, z), base = CH[c], 4 * (c % 2)
         mv = []
         for b in range(4):
-            out, src = T.vt[:, 4 * a + b:4 * z:4], T["ps%d" % (base + b)][:, 0:n]
+            out, src = T.vt[:, 4 * a + b:4 * z:4], T["ps%d" % (base + b)][:, 0:z - a]
             if b % 2 == 0:
-                need("v", last[b])
+                need("v", last[c, b])
                 mv.append(fin("sv", V.tensor_copy(out, src)))
             else:
-                need("s", last[b])
+                need("s", last[c, b])
                 mv.append(fin("ss", S.activation(out, src, COPY)))
             free[base + b] = mv[-1]
         need("v", *mv)
-        m_vq = fin("sv", V.quantize_mx(T.vq[:, a:z], T.vp[:, a:z], T.vt[:, 4 * a:4 * z]))
-        need("p", m_wq, m_vq)
-        my = []
+        m_vq[c] = fin("sv", V.quantize_mx(T.vq[:, a:z], T.vp[:, a:z], T.vt[:, 4 * a:4 * z]))
+
+    def product(c):
+        (a, z), base = CH[c], 4 * (c % 2)
+        need("p", m_wq, m_vq[c])
         for o in range(O):
-            my.append(fin("sp", P.matmul_mx(T["ps%d" % (base + o)][:, 0:n], T.wq[:, 128 * o:128 * o + 128],
-                                            T.wp[:, 128 * o:128 * o + 128], T.vq[:, a:z], T.vp[:, a:z], True, True)))
+            my[c, o] = fin("sp", P.matmul_mx(T["ps%d" % (base + o)][:, 0:z - a], T.wq[:, 128 * o:128 * o + 128],
+                                             T.wp[:, 128 * o:128 * o + 128], T.vq[:, a:z], T.vp[:, a:z], True, True))
+
+    def store(c):
+        (a, z), base = CH[c], 4 * (c % 2)
+        n = z - a
         for o in range(O):
             lo = TOK * o + a
             out, src = T.yt[:, lo:lo + n], T["ps%d" % (base + o)][:, 0:n]
             if o == 0:
-                need("v", my[o])
+                need("v", my[c, o])
                 mk = fin("sv", V.tensor_copy(out, src))
                 dq = "y"
             else:
-                need("s", my[o])
+                need("s", my[c, o])
                 mk = fin("ss", S.activation(out, src, COPY))
                 dq = "s" if c == len(CH) - 1 else "y"
             free[base + o] = mk
             need(dq, mk)
             fin("ly", Q[dq].dma_start(T.y[:, lo:lo + n], T.yt[:, lo:lo + n]), 16)
+
+    for c in range(len(CH)):
+        for i in range(4):
+            if c > 0 and i == CFG["WLAG"]:
+                product(c - 1)
+                store(c - 1)
+            decode(c, i)
+        tile(c)
+    product(len(CH) - 1)
+    store(len(CH) - 1)
     g.wait_ge(T.sem.sent, local[0])
     for sem in ("sv", "ss", "sp", "sg", "ly"):
         need("g", (sem, done[sem]))

@@ -6,25 +6,30 @@ HA = (1237, 1811, 947, 1543)
 HB = (40503, 12289, 58111, 3571)
 COPY = ActivationFunctionType.Copy
 CFG = {
-    "CH": [(0, 320), (320, 512)],
+    "CUT": (320, 320, 288, 288),
     "XOR": (2, 3, 1),
-    "NV": [[2, 2, 2], [2, 2, 1]],
+    "NV": [[2, 2, 1], [2, 2, 2]],
     "OV": [2, 1],
-    "WLAG": 2,
+    "SEQ": "00 01 02 03 t 10 11 w 12 13",
+    "PACK0": 0,
+    "LE": ((0, 8), (8, 12), (12, 16)),
 }
 
 SCRATCH = {
     "ids8": ("sbuf", [128, 32], "int32"),
-    "lst": ("sbuf", [128, 96], "int32"),
     "hx": ("sbuf", [128, 128], "int32"),
     "hh": ("sbuf", [128, 128], "int32"),
+    "mine": ("sbuf", [128, 256], "uint16"),
+    "mineo": ("sbuf", [128, 64], "uint16"),
+    "even": ("sbuf", [128, 192], "uint16"),
+    "odd": ("sbuf", [128, 192], "uint16"),
     "tbt": ("sbuf", [128, 4 * K], "bfloat16"),
     "wt": ("sbuf", [128, 512 * O], "bfloat16"),
     "wq": ("sbuf", [128, 128 * O], "float8_e4m3fn_x4"),
     "wp": ("sbuf", [128, 128 * O], "uint8"),
     "one": ("sbuf", [128, 128], "bfloat16"),
     "eye": ("sbuf", [128, 128], "bfloat16"),
-    "e": ("sbuf", [128, 2048], "bfloat16"),
+    "e": ("sbuf", [128, 528], "bfloat16"),
     "eq": ("sbuf", [128, 512], "float8_e4m3fn_x4"),
     "ep": ("sbuf", [128, 512], "uint8"),
     "vt": ("sbuf", [128, 4 * TOK], "bfloat16"),
@@ -32,8 +37,6 @@ SCRATCH = {
     "vp": ("sbuf", [128, TOK], "uint8"),
     "yt": ("sbuf", [128, O * TOK], "float32"),
 }
-for _t in range(4):
-    SCRATCH["off%d" % _t] = ("sbuf", [128, 128], "uint16")
 for _s in range(4):
     SCRATCH["gt%d" % _s] = ("sbuf", [128, 4 * TOK], "bfloat16")
     SCRATCH["gq%d" % _s] = ("sbuf", [128, TOK], "float8_e4m3fn_x4")
@@ -45,20 +48,23 @@ for _b in range(8):
     SCRATCH["ps%d" % _b] = ("psum", [128, 512], "float32")
 
 SEMAPHORES = ["sv", "ss", "sp", "sg", "li", "lt", "lw", "ly", "sent"] + \
-    ["la%d" % s for s in range(3)] + ["ar%d%d" % (s, c) for s in range(3) for c in range(4)]
+    ["la%d" % s for s in range(3)] + ["ar%d%d" % (s, c) for s in range(3) for c in range(2)]
 
 
 def rank_program(g, core, T, topo):
     r = T.rank_of(core)
     if r is None:
         return
-    CH, XOR = CFG["CH"], CFG["XOR"]
+    XOR = CFG["XOR"]
     V, S, P, Y = g.vector, g.scalar, g.tensor, g.sync
     Q = {"v": V, "s": S, "p": P, "g": g, "y": Y}
     peer = [r ^ XOR[s] for s in range(3)]
     pcore = [T.cores[p] for p in peer]
     eng = [topo.engines(core, c) for c in pcore]
     done, seen, local = {}, {}, [0]
+
+    def run(q, c):
+        return ((0, CFG["CUT"][q]), (CFG["CUT"][q], TOK))[c]
 
     def fin(sem, ins, n=1):
         ins.then_inc(T.sem[sem], n)
@@ -90,96 +96,110 @@ def rank_program(g, core, T, topo):
     m_one = fin("sv", V.memset(T.one[:], 1.0))
     need("g", m_one)
     m_eye = fin("sg", g.affine_select(T.eye[:], T.one[:], [[-1, 128]], AluOpType.is_equal, 0.0, 0, 1))
-    m = fin("sv", V.memset(T.e[:], 0.0))
-    need("v", m, m_eye)
+    need("v", fin("sv", V.memset(T.e[:], 0.0)), m_eye)
+    need("v", fin("sv", V.tensor_copy(T.e[:, 4:516:4], T.eye[:])))
     for b in range(4):
-        m = fin("sv", V.tensor_copy(T.e[:, 512 * b + b:512 * b + 512:4], T.eye[:]))
-    need("v", m)
-    m_e = fin("sv", V.quantize_mx(T.eq[:], T.ep[:], T.e[:]))
+        m_e = fin("sv", V.quantize_mx(T.eq[:, 128 * b:128 * b + 128], T.ep[:, 128 * b:128 * b + 128], T.e[:, 4 - b:516 - b]))
 
-    need("g", m_ids)
-    lists = [(s, es, T.ids8[:], T.lst[:, 32 * s:32 * s + 32], "la%d" % s)
-             for s, es in enumerate((eng[0][0:8], eng[1][8:12], eng[2][12:16]))]
-    send(lists[0:1])
-    send(lists[1:3])
-    m_la = [(x[4], len(x[1])) for x in lists]
+    tabs = peer + [r]
 
-    m_off = {}
+    def columns(s0, s1):
+        for s in range(s0, s1):
+            m = fin("sv", V.tensor_scalar(T.hx[:, 32 * s:32 * s + 32], T.ids8[:], HA[tabs[s]], HB[tabs[s]], AluOpType.mult, AluOpType.add))
+        need("v", m)
+        need("v", fin("sv", V.tensor_scalar(T.hh[:, 32 * s0:32 * s1], T.hx[:, 32 * s0:32 * s1], 3, 4 * (K - 1),
+                                            AluOpType.logical_shift_right, AluOpType.bitwise_and)))
 
-    def hashes(src, b0, b1, order):
-        c0, c1 = 32 * b0, 32 * b1
-        x, h = T.hx[:, c0:c1], T.hh[:, c0:c1]
-        need("v", fin("sv", V.tensor_scalar(x, src, HA[r], HB[r], AluOpType.mult, AluOpType.add)))
-        need("v", fin("sv", V.tensor_scalar(h, x, 3, 4 * (K - 1), AluOpType.logical_shift_right, AluOpType.bitwise_and)))
-        for t in order:
-            m3 = fin("sv", V.tensor_scalar(T["off%d" % t][:, c0:c1], h, t, None, AluOpType.add))
-            for k in range(b0, b1):
-                m_off[k, t] = m3
+    def evens(s):
+        h = T.hh[:, 32 * s:32 * s + 32]
+        fin("sv", V.tensor_copy(T.mine[:, 64 * s:64 * s + 32], h))
+        return fin("sv", V.tensor_scalar(T.mine[:, 64 * s + 32:64 * s + 64], h, 2, None, AluOpType.add))
+
+    def plus1(out, src, *marks):
+        need("v", *marks)
+        return fin("sv", V.tensor_scalar(out, src, 1, None, AluOpType.add))
+
+    def addresses(ss):
+        send([(s, eng[s][CFG["LE"][s][0]:CFG["LE"][s][1]], T.mine[:, 64 * s:64 * s + 64], T.even[:, 64 * s:64 * s + 64], "la%d" % s) for s in ss])
+
+    need("v", m_ids)
+    columns(0, 1)
+    need("g", evens(0))
+    addresses([0])
+    columns(1, 4)
+    m_ev = evens(3)
+    m_od = plus1(T.mineo[:], T.mine[:, 192:256], m_ev)
+    evens(1)
+    need("g", evens(2))
+    addresses([1, 2])
+    m_la = [("la%d" % s, z - a) for s, (a, z) in enumerate(CFG["LE"])]
+
+    m_off = {(0, 0): m_ev, (0, 1): m_od}
+    for s in range(3):
+        m_off[s + 1, 0] = m_la[s]
 
     def gather(k, c, nv):
-        a, z = CH[c]
-        o = 32 * k
+        a, z = run(tabs[k - 1], c)
         marks = []
-        for t in range(4):
+        for t in (0, 2, 1, 3):
+            if k == 0:
+                off, o = (T.mineo, 0) if t % 2 else (T.mine, 192)
+            else:
+                off, o = (T.odd if t % 2 else T.even), 64 * (k - 1)
+            o += 32 * (t // 2)
             out = T["gt%d" % k][:, 4 * a + t:4 * z:4]
-            src = T.tbt[:].indirect(T["off%d" % t][:, o + a // 16:o + z // 16])
-            if t < nv:
-                need("v", m_tb, m_off[k, t])
+            src = T.tbt[:].indirect(off[:, o + a // 16:o + z // 16])
+            q = "v" if t < nv else "s"
+            need(q, m_tb, m_off[k, t % 2])
+            if q == "v":
                 marks.append(fin("sv", V.tensor_copy(out, src)))
             else:
-                need("s", m_tb, m_off[k, t])
                 marks.append(fin("ss", S.activation(out, src, COPY)))
         return marks
 
     def pack(k, c, marks):
-        a, z = CH[c]
+        a, z = run(tabs[k - 1], c)
         need("v", *marks)
         return fin("sv", V.quantize_mx(T["gq%d" % k][:, a:z], T["gp%d" % k][:, a:z], T["gt%d" % k][:, 4 * a:4 * z]))
 
     m_own = {}
-    need("v", m_ids)
-    hashes(T.ids8[:], 0, 1, (2, 3, 0, 1))
-    early = len(CH) - 1
-    for c in range(early):
-        m_own[c] = pack(0, c, gather(0, c, CFG["OV"][c]))
+    own0 = gather(0, 0, CFG["OV"][0])
 
     arr = {}
-    for c, (a, z) in enumerate(CH):
+    for c in range(2):
         for s in range(3):
             k = s + 1
+            a, z = run(peer[s], c)
+            if c == 0 and s == CFG["PACK0"]:
+                m_own[0] = pack(0, 0, own0)
             if c == 0 and s == 0:
-                need("v", m_la[0])
-                hashes(T.lst[:, 0:32], 1, 2, (3, 2, 1, 0))
+                m_off[1, 1] = plus1(T.odd[:, 0:64], T.even[:, 0:64], m_la[0])
             marks = gather(k, c, CFG["NV"][c][s])
             if c == 0 and s == 0:
-                need("v", m_la[1], m_la[2])
-                hashes(T.lst[:, 32:96], 2, 4, (3, 2, 1, 0))
+                m_off[2, 1] = m_off[3, 1] = plus1(T.odd[:, 64:192], T.even[:, 64:192], m_la[1], m_la[2])
             need("g", pack(k, c, marks))
             sem = "ar%d%d" % (s, c)
             send([(s, eng[s], T["gq%d" % k][:, a:z].bitcast(dt.uint8), T["rq%d" % k][:, a:z].bitcast(dt.uint8), sem)])
             send([(s, eng[s], T["gp%d" % k][:, a:z], T["rp%d" % k][:, a:z], sem)])
             arr[peer[s], c] = (sem, 2 * len(eng[s]))
-    for c in range(early, len(CH)):
-        m_own[c] = pack(0, c, gather(0, c, CFG["OV"][c]))
+    m_own[1] = pack(0, 1, gather(0, 1, CFG["OV"][1]))
     need("v", m_w)
     m_wq = fin("sv", V.quantize_mx(T.wq[:], T.wp[:], T.wt[:]))
 
     order = [1, 0, 2, 3] if (r == 1 or r == 3) else [0, 1, 2, 3]
-    free, last, m_vq, my = {}, {}, {}, {}
+    last, m_vq, my = {}, {}, {}
 
     def decode(c, i):
-        (a, z), q, base = CH[c], order[i], 4 * (c % 2)
+        (a, z), q, base = run(r, c), order[i], 4 * c
         k = 0 if q == r else peer.index(q) + 1
         cq, cp, mk = (T.gq0, T.gp0, m_own[c]) if q == r else (T["rq%d" % k], T["rp%d" % k], arr[q, c])
         need("p", m_e, mk)
         for b in range(4):
-            if i == 0 and base + b in free:
-                need("p", free[base + b])
             last[c, b] = fin("sp", P.matmul_mx(T["ps%d" % (base + b)][:, 0:z - a], T.eq[:, 128 * b:128 * b + 128],
                                                T.ep[:, 128 * b:128 * b + 128], cq[:, a:z], cp[:, a:z], i == 0, i == 3))
 
     def tile(c):
-        (a, z), base = CH[c], 4 * (c % 2)
+        (a, z), base = run(r, c), 4 * c
         mv = []
         for b in range(4):
             out, src = T.vt[:, 4 * a + b:4 * z:4], T["ps%d" % (base + b)][:, 0:z - a]
@@ -189,19 +209,18 @@ def rank_program(g, core, T, topo):
             else:
                 need("s", last[c, b])
                 mv.append(fin("ss", S.activation(out, src, COPY)))
-            free[base + b] = mv[-1]
         need("v", *mv)
         m_vq[c] = fin("sv", V.quantize_mx(T.vq[:, a:z], T.vp[:, a:z], T.vt[:, 4 * a:4 * z]))
 
     def product(c):
-        (a, z), base = CH[c], 4 * (c % 2)
+        (a, z), base = run(r, c), 4 * c
         need("p", m_wq, m_vq[c])
         for o in range(O):
             my[c, o] = fin("sp", P.matmul_mx(T["ps%d" % (base + o)][:, 0:z - a], T.wq[:, 128 * o:128 * o + 128],
                                              T.wp[:, 128 * o:128 * o + 128], T.vq[:, a:z], T.vp[:, a:z], True, True))
 
     def store(c):
-        (a, z), base = CH[c], 4 * (c % 2)
+        (a, z), base = run(r, c), 4 * c
         n = z - a
         for o in range(O):
             lo = TOK * o + a
@@ -213,20 +232,21 @@ def rank_program(g, core, T, topo):
             else:
                 need("s", my[c, o])
                 mk = fin("ss", S.activation(out, src, COPY))
-                dq = "s" if c == len(CH) - 1 else "y"
-            free[base + o] = mk
+                dq = "s" if c == 1 else "y"
             need(dq, mk)
             fin("ly", Q[dq].dma_start(T.y[:, lo:lo + n], T.yt[:, lo:lo + n]), 16)
 
-    for c in range(len(CH)):
-        for i in range(4):
-            if c > 0 and i == CFG["WLAG"]:
-                product(c - 1)
-                store(c - 1)
-            decode(c, i)
-        tile(c)
-    product(len(CH) - 1)
-    store(len(CH) - 1)
+    for op in CFG["SEQ"].split():
+        if op == "t":
+            tile(0)
+        elif op == "w":
+            product(0)
+            store(0)
+        else:
+            decode(int(op[0]), int(op[1]))
+    tile(1)
+    product(1)
+    store(1)
     g.wait_ge(T.sem.sent, local[0])
     for sem in ("sv", "ss", "sp", "sg", "ly"):
         need("g", (sem, done[sem]))

from concourse.bass import DstId, RemoteDMATransfer
from concourse.mybir import dt, AluOpType, ActivationFunctionType

N, TOK, K, O = 4, 512, 512, 2
HA = (1237, 1811, 947, 1543)
HB = (40503, 12289, 58111, 3571)
COPY = ActivationFunctionType.Copy
CFG = {
    "CUT": (320, 320, 288, 288),
    "XOR": (2, 3, 1),
    "NV": [[2, 2, 1], [2, 2, 2]],
    "OV": [2, 1],
    "SEQ": "00 01 02 03 t 10 11 w 12 13",
    "PACK0": 0,
    "LE": ((0, 8), (8, 12), (12, 16)),
}

SCRATCH = {
    "ids8": ("sbuf", [128, 32], "int32"),
    "hx": ("sbuf", [128, 128], "int32"),
    "hh": ("sbuf", [128, 128], "int32"),
    "mine": ("sbuf", [128, 256], "uint16"),
    "mineo": ("sbuf", [128, 64], "uint16"),
    "even": ("sbuf", [128, 192], "uint16"),
    "odd": ("sbuf", [128, 192], "uint16"),
    "tbt": ("sbuf", [128, 4 * K], "bfloat16"),
    "wt": ("sbuf", [128, 512 * O], "bfloat16"),
    "wq": ("sbuf", [128, 128 * O], "float8_e4m3fn_x4"),
    "wp": ("sbuf", [128, 128 * O], "uint8"),
    "one": ("sbuf", [128, 128], "bfloat16"),
    "eye": ("sbuf", [128, 128], "bfloat16"),
    "e": ("sbuf", [128, 528], "bfloat16"),
    "eq": ("sbuf", [128, 512], "float8_e4m3fn_x4"),
    "ep": ("sbuf", [128, 512], "uint8"),
    "vt": ("sbuf", [128, 4 * TOK], "bfloat16"),
    "vq": ("sbuf", [128, TOK], "float8_e4m3fn_x4"),
    "vp": ("sbuf", [128, TOK], "uint8"),
    "yt": ("sbuf", [128, O * TOK], "float32"),
}
for _s in range(4):
    SCRATCH["gt%d" % _s] = ("sbuf", [128, 4 * TOK], "bfloat16")
    SCRATCH["gq%d" % _s] = ("sbuf", [128, TOK], "float8_e4m3fn_x4")
    SCRATCH["gp%d" % _s] = ("sbuf", [128, TOK], "uint8")
for _s in range(1, 4):
    SCRATCH["rq%d" % _s] = ("sbuf", [128, TOK], "float8_e4m3fn_x4")
    SCRATCH["rp%d" % _s] = ("sbuf", [128, TOK], "uint8")
for _b in range(8):
    SCRATCH["ps%d" % _b] = ("psum", [128, 512], "float32")

SEMAPHORES = ["sv", "ss", "sp", "sg", "li", "lt", "lw", "ly", "sent"] + \
    ["la%d" % s for s in range(3)] + ["ar%d%d" % (s, c) for s in range(3) for c in range(2)]


def rank_program(g, core, T, topo):
    r = T.rank_of(core)
    if r is None:
        return
    XOR = CFG["XOR"]
    V, S, P, Y = g.vector, g.scalar, g.tensor, g.sync
    Q = {"v": V, "s": S, "p": P, "g": g, "y": Y}
    peer = [r ^ XOR[s] for s in range(3)]
    pcore = [T.cores[p] for p in peer]
    eng = [topo.engines(core, c) for c in pcore]
    done, seen, local = {}, {}, [0]

    def run(q, c):
        return ((0, CFG["CUT"][q]), (CFG["CUT"][q], TOK))[c]

    def fin(sem, ins, n=1):
        ins.then_inc(T.sem[sem], n)
        done[sem] = done.get(sem, 0) + n
        return (sem, done[sem])

    def need(q, *marks):
        for sem, n in marks:
            if seen.get((q, sem), 0) < n:
                Q[q].wait_ge(T.sem[sem], n)
                seen[(q, sem)] = n

    def send(items):
        tr = []
        for s, es, src, dst, sem in items:
            rid, pid, _ = topo.addr(pcore[s])
            tr.append(RemoteDMATransfer(dst_ids=[DstId(rid=rid, pnc=pid)], dma_engine_mask=sum(1 << e for e in es),
                                        remote_sem=T.sem[sem], srcs=[src], dsts=[dst]))
            local[0] += len(es)
        g.remote_dma_fused(tr, local_sem=T.sem.sent)

    for i in range(4):
        fin("li", Y.dma_start(T.ids8[16 * i:16 * i + 16, :], T.ids[:, :]), 16)
        j = i + 4
        m_ids = fin("li", S.dma_start(T.ids8[16 * j:16 * j + 16, :], T.ids[:, :]), 16)
    m_tb = fin("lt", Y.dma_start(T.tbt[:], T.tb[:, :]), 16)
    m_w = fin("lw", Y.dma_start(T.wt[:], T.w[:, :]), 16)

    m_one = fin("sv", V.memset(T.one[:], 1.0))
    need("g", m_one)
    m_eye = fin("sg", g.affine_select(T.eye[:], T.one[:], [[-1, 128]], AluOpType.is_equal, 0.0, 0, 1))
    need("v", fin("sv", V.memset(T.e[:], 0.0)), m_eye)
    need("v", fin("sv", V.tensor_copy(T.e[:, 4:516:4], T.eye[:])))
    for b in range(4):
        m_e = fin("sv", V.quantize_mx(T.eq[:, 128 * b:128 * b + 128], T.ep[:, 128 * b:128 * b + 128], T.e[:, 4 - b:516 - b]))

    tabs = peer + [r]

    def columns(s0, s1):
        for s in range(s0, s1):
            m = fin("sv", V.tensor_scalar(T.hx[:, 32 * s:32 * s + 32], T.ids8[:], HA[tabs[s]], HB[tabs[s]], AluOpType.mult, AluOpType.add))
        need("v", m)
        need("v", fin("sv", V.tensor_scalar(T.hh[:, 32 * s0:32 * s1], T.hx[:, 32 * s0:32 * s1], 3, 4 * (K - 1),
                                            AluOpType.logical_shift_right, AluOpType.bitwise_and)))

    def evens(s):
        h = T.hh[:, 32 * s:32 * s + 32]
        fin("sv", V.tensor_copy(T.mine[:, 64 * s:64 * s + 32], h))
        return fin("sv", V.tensor_scalar(T.mine[:, 64 * s + 32:64 * s + 64], h, 2, None, AluOpType.add))

    def plus1(out, src, *marks):
        need("v", *marks)
        return fin("sv", V.tensor_scalar(out, src, 1, None, AluOpType.add))

    def addresses(ss):
        send([(s, eng[s][CFG["LE"][s][0]:CFG["LE"][s][1]], T.mine[:, 64 * s:64 * s + 64], T.even[:, 64 * s:64 * s + 64], "la%d" % s) for s in ss])

    need("v", m_ids)
    columns(0, 1)
    need("g", evens(0))
    addresses([0])
    columns(1, 4)
    m_ev = evens(3)
    m_od = plus1(T.mineo[:], T.mine[:, 192:256], m_ev)
    evens(1)
    need("g", evens(2))
    addresses([1, 2])
    m_la = [("la%d" % s, z - a) for s, (a, z) in enumerate(CFG["LE"])]

    m_off = {(0, 0): m_ev, (0, 1): m_od}
    for s in range(3):
        m_off[s + 1, 0] = m_la[s]

    def gather(k, c, nv):
        a, z = run(tabs[k - 1], c)
        marks = []
        for t in (0, 2, 1, 3):
            if k == 0:
                off, o = (T.mineo, 0) if t % 2 else (T.mine, 192)
            else:
                off, o = (T.odd if t % 2 else T.even), 64 * (k - 1)
            o += 32 * (t // 2)
            out = T["gt%d" % k][:, 4 * a + t:4 * z:4]
            src = T.tbt[:].indirect(off[:, o + a // 16:o + z // 16])
            q = "v" if t < nv else "s"
            need(q, m_tb, m_off[k, t % 2])
            if q == "v":
                marks.append(fin("sv", V.tensor_copy(out, src)))
            else:
                marks.append(fin("ss", S.activation(out, src, COPY)))
        return marks

    def pack(k, c, marks):
        a, z = run(tabs[k - 1], c)
        need("v", *marks)
        return fin("sv", V.quantize_mx(T["gq%d" % k][:, a:z], T["gp%d" % k][:, a:z], T["gt%d" % k][:, 4 * a:4 * z]))

    m_own = {}
    own0 = gather(0, 0, CFG["OV"][0])

    arr = {}
    for c in range(2):
        for s in range(3):
            k = s + 1
            a, z = run(peer[s], c)
            if c == 0 and s == CFG["PACK0"]:
                m_own[0] = pack(0, 0, own0)
            if c == 0 and s == 0:
                m_off[1, 1] = plus1(T.odd[:, 0:64], T.even[:, 0:64], m_la[0])
            marks = gather(k, c, CFG["NV"][c][s])
            if c == 0 and s == 0:
                m_off[2, 1] = m_off[3, 1] = plus1(T.odd[:, 64:192], T.even[:, 64:192], m_la[1], m_la[2])
            need("g", pack(k, c, marks))
            sem = "ar%d%d" % (s, c)
            send([(s, eng[s], T["gq%d" % k][:, a:z].bitcast(dt.uint8), T["rq%d" % k][:, a:z].bitcast(dt.uint8), sem)])
            send([(s, eng[s], T["gp%d" % k][:, a:z], T["rp%d" % k][:, a:z], sem)])
            arr[peer[s], c] = (sem, 2 * len(eng[s]))
    m_own[1] = pack(0, 1, gather(0, 1, CFG["OV"][1]))
    need("v", m_w)
    m_wq = fin("sv", V.quantize_mx(T.wq[:], T.wp[:], T.wt[:]))

    order = [1, 0, 2, 3] if (r == 1 or r == 3) else [0, 1, 2, 3]
    last, m_vq, my = {}, {}, {}

    def decode(c, i):
        (a, z), q, base = run(r, c), order[i], 4 * c
        k = 0 if q == r else peer.index(q) + 1
        cq, cp, mk = (T.gq0, T.gp0, m_own[c]) if q == r else (T["rq%d" % k], T["rp%d" % k], arr[q, c])
        need("p", m_e, mk)
        for b in range(4):
            last[c, b] = fin("sp", P.matmul_mx(T["ps%d" % (base + b)][:, 0:z - a], T.eq[:, 128 * b:128 * b + 128],
                                               T.ep[:, 128 * b:128 * b + 128], cq[:, a:z], cp[:, a:z], i == 0, i == 3))

    def tile(c):
        (a, z), base = run(r, c), 4 * c
        mv = []
        for b in range(4):
            out, src = T.vt[:, 4 * a + b:4 * z:4], T["ps%d" % (base + b)][:, 0:z - a]
            if b % 2 == 0:
                need("v", last[c, b])
                mv.append(fin("sv", V.tensor_copy(out, src)))
            else:
                need("s", last[c, b])
                mv.append(fin("ss", S.activation(out, src, COPY)))
        need("v", *mv)
        m_vq[c] = fin("sv", V.quantize_mx(T.vq[:, a:z], T.vp[:, a:z], T.vt[:, 4 * a:4 * z]))

    def product(c):
        (a, z), base = run(r, c), 4 * c
        need("p", m_wq, m_vq[c])
        for o in range(O):
            my[c, o] = fin("sp", P.matmul_mx(T["ps%d" % (base + o)][:, 0:z - a], T.wq[:, 128 * o:128 * o + 128],
                                             T.wp[:, 128 * o:128 * o + 128], T.vq[:, a:z], T.vp[:, a:z], True, True))

    def store(c):
        (a, z), base = run(r, c), 4 * c
        n = z - a
        for o in range(O):
            lo = TOK * o + a
            out, src = T.yt[:, lo:lo + n], T["ps%d" % (base + o)][:, 0:n]
            if o == 0:
                need("v", my[c, o])
                mk = fin("sv", V.tensor_copy(out, src))
                dq = "y"
            else:
                need("s", my[c, o])
                mk = fin("ss", S.activation(out, src, COPY))
                dq = "s" if c == 1 else "y"
            need(dq, mk)
            fin("ly", Q[dq].dma_start(T.y[:, lo:lo + n], T.yt[:, lo:lo + n]), 16)

    for op in CFG["SEQ"].split():
        if op == "t":
            tile(0)
        elif op == "w":
            product(0)
            store(0)
        else:
            decode(int(op[0]), int(op[1]))
    tile(1)
    product(1)
    store(1)
    g.wait_ge(T.sem.sent, local[0])
    for sem in ("sv", "ss", "sp", "sg", "ly"):
        need("g", (sem, done[sem]))
